import numpy as np
CORES = [0,1,2,3,4,5,6,7,8,9,10,11,12,13,14,15,16,17,18,19,20,21,22,23,24,25,26,27,28,29,30,31,32,33,34,35,36,37,38,39,40,41,42,43,44,45,46,47,56,57,58,59,60,61,62,63,64,65,66,67,68,69,70,71,72,73,74,75,76,77,78,79,80,81,82,83,84,85,86,87,88,89,90,91,92,93,94,95,96,97,98,99,100,101,102,103,104,105,106,107,108,109,110,111,112,113,114,115,116,117,118,119,120,121,122,123,124,125,126,127,128,129,130,131,132,133,134,135,136,137,138,139,140,141,142,143,144,145,146,147,148,149,150,151,152,153,154,155,156,157,158,159,160,161,162,163,164,165,166,167,168,169,170,171,172,173,174,175,176,177,178,179,180,181,182,183,184,185,186,187,188,189,190,191,192,193,194,195,196,197,198,199,200,201,202,203,204,205,206,207,208,209,210,211,212,213,214,215,216,217,218,219,220,221,222,223,224,225,226,227,228,229,230,231,232,233,234,235,236,237,238,239,240,241,242,243,244,245,246,247,248,249,250,251,252,253,254,255]
N = 248
DEAD = {"mate_links":[[6,0],[6,1]],"switch_ports":[],"chips":[6]}
def setup_inputs(rng):
    return {"x": rng.standard_normal((N, 128, 16), dtype=np.float32)}
def reference(x):
    g = np.concatenate(list(x), axis=1)
    return {"y": np.broadcast_to(g, (N,) + g.shape)}

@@ -1,0 +1,129 @@
+import concourse.bass as bass
+
+BLK = 16
+NRANK = 248
+SCRATCH = {
+    "G": ("sbuf", [128, NRANK * BLK], "float32"),
+}
+SEMAPHORES = ["ld", "sent", "a1", "a2", "a3", "a4"]
+MCORES = (0, 1, 4, 5)
+NCORES = (2, 3, 6, 7)
+CACHE = {}
+
+
+def make_sends(cores, dead):
+    rank = {c: i for i, c in enumerate(cores)}
+    chips = sorted({c // 8 for c in cores})
+    lone = [g for g in chips if (g ^ 1) not in chips]
+    first = {g: rank[8 * g] for g in chips}
+    owner = {}
+    segs = {}
+    order = (0, 2, 1, 3, 4, 6, 5, 7)
+    for g in chips:
+        hole = {first[g] // 2 + i for i in range(4)}
+        if g not in lone:
+            hole |= {first[g ^ 1] // 2 + i for i in range(4)}
+        seq = [p for p in range(NRANK // 2) if p not in hole]
+        pos = 0
+        for j in order:
+            n = 15 if (g in lone or j in NCORES) else 14
+            mine = seq[pos:pos + n]
+            pos += n
+            runs = []
+            for p in mine:
+                owner[g, p] = 8 * g + j
+                if runs and runs[-1][0] + runs[-1][1] == 2 * p:
+                    runs[-1][1] += 2
+                else:
+                    runs.append([2 * p, 2])
+            segs[8 * g + j] = runs
+        assert pos == len(seq)
+    sends = []
+    for g in chips:
+        peers = [d for d in chips if d != g and d % 2 == g % 2]
+        for j in range(8):
+            c = 8 * g + j
+            on = [8 * g + k for k in range(8) if k != j]
+            sends.append((1, c, rank[c], 1, on))
+            if g in lone:
+                sends.append((1, c, rank[c], 1, [owner[d, rank[c] // 2] for d in peers]))
+            for b0, n in segs[c]:
+                sends.append((4, c, b0, n, on))
+        if g in lone:
+            continue
+        m = g ^ 1
+        for i in range(4):
+            p = first[g] // 2 + i
+            sends.append((2, 8 * g + NCORES[i], 2 * p, 2, [8 * m + MCORES[i]] + [owner[d, p] for d in peers]))
+            q = first[m] // 2 + i
+            c = 8 * g + MCORES[i]
+            sends.append((3, c, 2 * q, 2, [owner[d, q] for d in peers]))
+            sends.append((3, c, 2 * q, 2, [8 * g + k for k in range(8) if k != MCORES[i]]))
+        for l in lone:
+            if l % 2 == g % 2:
+                for i in range(4):
+                    p = first[l] // 2 + i
+                    sends.append((2, owner[g, p], 2 * p, 2, [owner[m, p]]))
+    return sends
+
+
+def compile_sends(sends):
+    calls = {}
+    for hop, src, b0, n, dsts in sends:
+        for k in range(0, len(dsts), 16):
+            calls.setdefault((src, hop, n), []).append((b0, list(dsts[k:k + 16])))
+    prog = {}
+    arrive = {}
+    sent = {}
+    for (src, hop, n), trs in sorted(calls.items()):
+        off = [tr for tr in trs if any(d // 8 != src // 8 for d in tr[1])]
+        on = [tr for tr in trs if tr not in off]
+        out = []
+        for group, base in ((off, 0), (on, 8)):
+            if not group:
+                continue
+            assert len(group) <= 8
+            e = 8
+            while e * len(group) > 8:
+                e //= 2
+            for i, (b0, dsts) in enumerate(group):
+                mask = ((1 << e) - 1) << (base + i * e)
+                out.append((b0, dsts, mask, e))
+                sent[src] = sent.get(src, 0) + e
+                for d in dsts:
+                    arrive[d, hop] = arrive.get((d, hop), 0) + e
+        prog.setdefault(src, {}).setdefault(hop, []).append((n, out))
+    return prog, arrive, sent
+
+
+def rank_program(g, core, T, topo):
+    rank = T.rank_of(core)
+    if rank is None:
+        return
+    if "plan" not in CACHE:
+        CACHE["plan"] = compile_sends(make_sends(list(T.cores), T.tables["DEAD"]))
+    prog, arrive, sent = CACHE["plan"]
+    G = T.G
+    sems = {1: T.sem.a1, 2: T.sem.a2, 3: T.sem.a3, 4: T.sem.a4}
+    g.dma_start(G[:, rank * BLK:(rank + 1) * BLK], T.x[:, :]).then_inc(T.sem.ld, 16)
+    g.wait_ge(T.sem.ld, 16)
+    for hop in (1, 2, 3, 4):
+        if hop > 1 and arrive.get((core, hop - 1), 0):
+            g.wait_ge(sems[hop - 1], arrive[core, hop - 1])
+        for n, trs in prog.get(core, {}).get(hop, []):
+            lst = []
+            for b0, dsts, mask, e in trs:
+                ap = G[:, b0 * BLK:(b0 + n) * BLK]
+                ids = []
+                for d in dsts:
+                    rid, pid = topo.addr(d, core)
+                    ids.append(bass.DstId(rid=rid, pnc=pid))
+                lst.append(bass.RemoteDMATransfer(dst_ids=ids, dma_engine_mask=mask, remote_sem=sems[hop],
+                                                  srcs=[ap], dsts=[ap for d in dsts]))
+            g.remote_dma_fused(lst, local_sem=T.sem.sent)
+    if arrive.get((core, 4), 0):
+        g.wait_ge(sems[4], arrive[core, 4])
+    if sent.get(core, 0):
+        g.wait_ge(T.sem.sent, sent[core])
+    g.dma_start(T.y[:, :], G[:, :]).then_inc(T.sem.ld, 16)
+    g.wait_ge(T.sem.ld, 32)

@@ -2,69 +2,327 @@ import concourse.bass as bass
 
 BLK = 16
 NRANK = 248
+UB = 4
 SCRATCH = {
     "G": ("sbuf", [128, NRANK * BLK], "float32"),
 }
 SEMAPHORES = ["ld", "sent", "a1", "a2", "a3", "a4"]
-MCORES = (0, 1, 4, 5)
-NCORES = (2, 3, 6, 7)
+LIMIT = 256
+PORT = 120
+SPARE = 4
+SPARE_LONE = 10
+ORDER = ((0, 0), (1, 0), (0, 1), (1, 1))
 CACHE = {}
+
+
+def solve(segs, labels, base, typ, nat, pin, limit):
+    fwd = 7 * UB
+    haslab = [any(u in labels for u in s) for s in segs]
+    total = sum(len(s) for s in segs)
+
+    def fits(j, us, load):
+        for u in us:
+            if u in labels:
+                t, hf, extra = labels[u]
+                if typ[j] != t or (hf is not None and j // 4 != hf):
+                    return None
+                load += extra
+        load += fwd * len(us)
+        return load if load <= limit else None
+
+    def search(twos, helpers):
+        load = list(base)
+        for hf in (0, 1):
+            load[4 * hf + 2] += UB * (pin if helpers else nat[hf])
+        runs = {}
+        failed = set()
+
+        def rec(si, off, last, used, pend, two, left):
+            if si == len(segs):
+                if used != 255 or pend is not None:
+                    return False
+                return not helpers or all(
+                    sum((limit - load[j]) // UB for j in range(4 * hf, 4 * hf + 4)) >= nat[hf] - pin for hf in (0, 1))
+            seg = segs[si]
+            if off == len(seg):
+                return rec(si + 1, 0, -1, used, pend, two, left)
+            key = (si, off, last, used, pend, two)
+            if helpers:
+                key += (sum(load[:4]),)
+            if key in failed:
+                return False
+            room = len(seg) - off
+            free = [j for j in range(8) if not used >> j & 1]
+            slack = sum((limit - load[j]) // fwd for j in free) + (pend[1] if pend else 0) - left
+            if slack >= 0:
+                if pend and pend[1] <= room:
+                    j, w = pend
+                    old = load[j]
+                    new = fits(j, seg[off:off + w], old)
+                    if new is not None:
+                        load[j] = new
+                        runs[j].append((seg[off], w))
+                        if rec(si, off + w, last, used, None, two, left - w):
+                            return True
+                        runs[j].pop()
+                        load[j] = old
+                for j in free:
+                    if not haslab[si] and j < last:
+                        continue
+                    old = load[j]
+                    cap = (limit - old) // fwd
+                    for w in range(min(cap, room), max(0, cap - slack - 1), -1):
+                        new = fits(j, seg[off:off + w], old)
+                        if new is None:
+                            continue
+                        load[j] = new
+                        runs[j] = [(seg[off], w)]
+                        if rec(si, off + w, j, used | 1 << j, pend, two, left - w):
+                            return True
+                    if two < twos and pend is None:
+                        for w in range(min(cap // 2, room), 1, -1):
+                            if 2 * w < cap - slack:
+                                break
+                            new = fits(j, seg[off:off + w], old)
+                            if new is None or new + fwd * w > limit:
+                                continue
+                            load[j] = new
+                            runs[j] = [(seg[off], w)]
+                            if rec(si, off + w, j, used | 1 << j, (j, w), two + 1, left - w):
+                                return True
+                    load[j] = old
+                    runs.pop(j, None)
+            failed.add(key)
+            return False
+
+        return runs if rec(0, 0, -1, 0, None, 0, total) else None
+
+    for n, cost in enumerate(ORDER):
+        if pin == 0 and cost[1] == 0:
+            continue
+        runs = search(cost[0], cost[1] == 1)
+        if runs is not None:
+            return n, runs
+    return None, None
 
 
 def make_sends(cores, dead):
     rank = {c: i for i, c in enumerate(cores)}
     chips = sorted({c // 8 for c in cores})
-    lone = [g for g in chips if (g ^ 1) not in chips]
-    first = {g: rank[8 * g] for g in chips}
+    nunit = len(cores) // UB
+    unit = {(g, hf): rank[8 * g + 4 * hf] // UB for g in chips for hf in (0, 1)}
+    mate = {g: (g ^ 1 if g ^ 1 in chips else None) for g in chips}
+    peers = {g: [d for d in chips if d != g and d // 16 == g // 16 and d % 2 == g % 2] for g in chips}
+    lone = [g for g in chips if mate[g] is None]
+    relay = {(g // 16, g % 2): g for g in lone}
+    F = {g: {} for g in chips}
+    orphans = []
+    for g in chips:
+        p = g ^ 16
+        for hf in (0, 1):
+            if p in chips and mate[p] is not None:
+                F[p][hf] = unit[g, hf]
+            else:
+                orphans.append((unit[g, hf], hf, p // 16, g % 2, True))
+            if mate[g] is None:
+                orphans.append((unit[g, hf], hf, g // 16, g % 2, False))
+
+    def layout(g, labels, shed):
+        P = len(peers[g])
+        m = mate[g]
+        hole = {unit[g, 0], unit[g, 1]} | set(F[g].values())
+        base = [3 + 1 + (1 if m is None else 0)] * 8
+        typ = ["L" if (m is None or j % 4 < 2) else "E" for j in range(8)]
+        if m is not None:
+            hole |= {unit[m, 0], unit[m, 1]} | set(F[m].values())
+            for hf in (0, 1):
+                if hf in F[g]:
+                    base[4 * hf + 3] += UB * (1 + (1 if hf in shed else P) + 7)
+                base[4 * hf] += UB * (P + 7)
+                if hf in F[m]:
+                    base[4 * hf + 1] += UB * (P + 7)
+            nat = [1 + P + 4] * 2
+            pin = 5 + ((g // 16, g % 2) in relay)
+            if len(F[g]) + len(F[m]) < 4:
+                for j in (0, 1, 4, 5):
+                    base[j] += UB * SPARE
+        else:
+            nat = [P - 1 + 4 + SPARE_LONE] * 2
+            pin = 0
+        segs = []
+        for u in range(nunit):
+            if u in hole:
+                continue
+            if segs and segs[-1][-1] == u - 1:
+                segs[-1].append(u)
+            else:
+                segs.append([u])
+        return segs, labels, base, typ, nat, pin
+
+    def adoption(a, orphan):
+        u, hf, h, q, foreign = orphan
+        m = mate[a]
+        ra, rm = (h, q) in relay, (h, 1 - q) in relay
+        ea = UB * ((1 + (1 if ra else len(peers[a]))) if foreign else 1)
+        la = {u: ("E", hf if ra and foreign else None, ea)}
+        lm = {u: ("L", hf if rm else None, UB * len(peers[m]))}
+        return (la, set()), (lm, {hf} if rm else set())
+
+    plain = {g: solve(*layout(g, {}, set()), LIMIT) for g in chips}
+    cand = {}
+    for i, o in enumerate(orphans):
+        for a in chips:
+            if a // 16 == o[2] and a % 2 == o[3] and mate[a] is not None:
+                (la, sa), (lm, sm) = adoption(a, o)
+                ca = solve(*layout(a, la, sa), LIMIT)
+                cm = solve(*layout(mate[a], lm, sm), LIMIT)
+                if ca[0] is not None and cm[0] is not None:
+                    cand[i, a] = (ca, cm, ca[0] + cm[0] - plain[a][0] - plain[mate[a]][0])
+    pick = {"cost": None, "sel": None}
+
+    def match(i, sel, cost):
+        if pick["cost"] is not None and cost >= pick["cost"]:
+            return
+        if i == len(orphans):
+            pick["cost"], pick["sel"] = cost, dict(sel)
+            return
+        for a in chips:
+            if (i, a) in cand and a not in sel.values() and mate[a] not in sel.values():
+                sel[i] = a
+                match(i + 1, sel, cost + cand[i, a][2])
+                del sel[i]
+
+    match(0, {}, 0)
+    adopt = pick["sel"]
+    runs = {g: plain[g][1] for g in chips}
+    shed = {g: set() for g in chips}
+    for i, a in adopt.items():
+        runs[a], runs[mate[a]] = cand[i, a][0][1], cand[i, a][1][1]
+        shed[mate[a]] = adoption(a, orphans[i])[1][1]
+    for r in lone:
+        lab = {}
+        for i, a in adopt.items():
+            u, hf, h, q, foreign = orphans[i]
+            if foreign and relay.get((h, q)) == r:
+                lab[u] = ("L", hf, UB * (len(peers[r]) - 1))
+            if relay.get((h, 1 - q)) == r:
+                lab[F[mate[a]][hf]] = ("L", hf, UB * (len(peers[r]) - 1))
+        runs[r] = solve(*layout(r, lab, set()), LIMIT)[1]
     owner = {}
-    segs = {}
-    order = (0, 2, 1, 3, 4, 6, 5, 7)
     for g in chips:
-        hole = {first[g] // 2 + i for i in range(4)}
-        if g not in lone:
-            hole |= {first[g ^ 1] // 2 + i for i in range(4)}
-        seq = [p for p in range(NRANK // 2) if p not in hole]
-        pos = 0
-        for j in order:
-            n = 15 if (g in lone or j in NCORES) else 14
-            mine = seq[pos:pos + n]
-            pos += n
-            runs = []
-            for p in mine:
-                owner[g, p] = 8 * g + j
-                if runs and runs[-1][0] + runs[-1][1] == 2 * p:
-                    runs[-1][1] += 2
-                else:
-                    runs.append([2 * p, 2])
-            segs[8 * g + j] = runs
-        assert pos == len(seq)
-    sends = []
+        for j, rs in runs[g].items():
+            for u0, w in rs:
+                for u in range(u0, u0 + w):
+                    owner[g, u] = 8 * g + j
+
+    jobs = {}
+    load = {c: 0 for c in cores}
+    pout, pin = {}, {}
+    chipout = {g: 0 for g in chips}
+
+    def add(hop, src, b0, n, dsts):
+        jobs.setdefault((hop, src, b0, n), []).extend(dsts)
+        sg, sh = src // 8, src % 8 // 4
+        for d in dsts:
+            load[src] += n
+            if d // 8 != sg:
+                chipout[sg] += n
+                if d // 8 != mate[sg]:
+                    pout[sg, sh] = pout.get((sg, sh), 0) + n
+                    pin[d // 8, sh] = pin.get((d // 8, sh), 0) + n
+
+    def sibs(c, half=None):
+        return [8 * (c // 8) + k for k in range(8) if 8 * (c // 8) + k != c and (half is None or k // 4 == half)]
+
+    land = {}
     for g in chips:
-        peers = [d for d in chips if d != g and d % 2 == g % 2]
+        for hf, u in F[g].items():
+            land.setdefault(u, []).append(8 * g + 4 * hf + 3)
+    for i, a in adopt.items():
+        land.setdefault(orphans[i][0], []).append(owner[a, orphans[i][0]])
+    for g in chips:
+        m = mate[g]
         for j in range(8):
             c = 8 * g + j
-            on = [8 * g + k for k in range(8) if k != j]
-            sends.append((1, c, rank[c], 1, on))
-            if g in lone:
-                sends.append((1, c, rank[c], 1, [owner[d, rank[c] // 2] for d in peers]))
-            for b0, n in segs[c]:
-                sends.append((4, c, b0, n, on))
-        if g in lone:
+            add(1, c, rank[c], 1, sibs(c, j // 4) + land[unit[g, j // 4]])
+            for u0, w in runs[g][j]:
+                add(4, c, UB * u0, UB * w, sibs(c))
+        if m is None:
             continue
-        m = g ^ 1
-        for i in range(4):
-            p = first[g] // 2 + i
-            sends.append((2, 8 * g + NCORES[i], 2 * p, 2, [8 * m + MCORES[i]] + [owner[d, p] for d in peers]))
-            q = first[m] // 2 + i
-            c = 8 * g + MCORES[i]
-            sends.append((3, c, 2 * q, 2, [owner[d, q] for d in peers]))
-            sends.append((3, c, 2 * q, 2, [8 * g + k for k in range(8) if k != MCORES[i]]))
-        for l in lone:
-            if l % 2 == g % 2:
-                for i in range(4):
-                    p = first[l] // 2 + i
-                    sends.append((2, owner[g, p], 2 * p, 2, [owner[m, p]]))
-    return sends
+        r = relay.get((g // 16, g % 2))
+        for hf in (0, 1):
+            if hf in F[g]:
+                u, c = F[g][hf], 8 * g + 4 * hf + 3
+                if hf in shed[g]:
+                    add(2, c, UB * u, UB, [8 * m + 4 * hf + 1, owner[r, u]] + sibs(c))
+                    add(3, owner[r, u], UB * u, UB, [owner[d, u] for d in peers[g] if d != r])
+                else:
+                    add(2, c, UB * u, UB, [8 * m + 4 * hf + 1] + [owner[d, u] for d in peers[g]] + sibs(c))
+            for u, c in ((unit[m, hf], 8 * g + 4 * hf), (F[m].get(hf), 8 * g + 4 * hf + 1)):
+                if u is not None:
+                    add(3, c, UB * u, UB, [owner[d, u] for d in peers[g]] + sibs(c))
+    skip = {}
+    for i, a in adopt.items():
+        u, hf, h, q, foreign = orphans[i]
+        m = mate[a]
+        r = relay.get((h, q))
+        dsts = [owner[m, u]]
+        if foreign and r is not None:
+            dsts.append(owner[r, u])
+            add(3, owner[r, u], UB * u, UB, [owner[d, u] for d in peers[a] if d != r])
+        elif foreign:
+            dsts += [owner[d, u] for d in peers[a]]
+        else:
+            skip[u] = a
+        add(2, owner[a, u], UB * u, UB, dsts)
+        add(3, owner[m, u], UB * u, UB, [owner[d, u] for d in peers[m]])
+    for g in chips:
+        m = mate[g]
+        r = relay.get((g // 16, g % 2))
+        for hf in (0, 1):
+            u = unit[g, hf]
+            other = [8 * g + 4 * (1 - hf) + k for k in range(4)]
+            if m is None:
+                for d in other + [owner[d, u] for d in peers[g] if d != skip.get(u)]:
+                    c = min((8 * g + 4 * hf + k for k in range(4)), key=lambda k: load[k])
+                    add(3, c, UB * u, UB, [d])
+                continue
+            en = 8 * g + 4 * hf + 2
+            add(2, en, UB * u, UB, [8 * m + 4 * hf] + other + ([owner[r, u]] if r is not None else []))
+            for d in peers[g]:
+                if d == r:
+                    continue
+                if pout.get((g, hf), 0) + UB > PORT:
+                    c = min((8 * g + 4 * (1 - hf) + k for k in (0, 1)), key=lambda k: load[k])
+                elif load[en] + UB <= LIMIT:
+                    c = en
+                else:
+                    c = min((8 * g + 4 * hf + k for k in (0, 1, 3)), key=lambda k: load[k])
+                add(2 if c % 4 > 1 else 3, c, UB * u, UB, [owner[d, u]])
+    for h, q in sorted({(g // 16, g % 2) for g in chips}):
+        r = min((g for g in chips if (g // 16, g % 2) == (h, q)), key=lambda g: chipout[g])
+        while True:
+            o = max(peers[r], key=lambda d: chipout[d])
+            if chipout[o] - UB < chipout[r] + UB:
+                break
+            opts = []
+            for (hop, src, b0, n), dsts in jobs.items():
+                k = owner.get((r, b0 // UB))
+                if hop == 2 and src // 8 == o and n == UB and k in dsts and (mate[r] is None or k % 4 < 2):
+                    rest = [d for d in dsts if d // 8 in peers[o] and d // 8 != r
+                            and pin[d // 8, k % 8 // 4] + UB <= PORT]
+                    if rest and load[k] + UB <= LIMIT and pout[r, k % 8 // 4] + UB <= PORT:
+                        opts.append(((3, k, b0, n) not in jobs, -load[src], load[k], src, b0, rest[-1], k))
+            if not opts:
+                break
+            src, b0, d, k = min(opts)[3:]
+            jobs[2, src, b0, UB].remove(d)
+            load[src] -= UB
+            chipout[o] -= UB
+            pout[o, src % 8 // 4] -= UB
+            pin[d // 8, src % 8 // 4] -= UB
+            add(3, k, b0, UB, [d])
+    return [(hop, src, b0, n, dsts) for (hop, src, b0, n), dsts in sorted(jobs.items()) if dsts]
 
 
 def compile_sends(sends):

@@ -9,7 +9,7 @@ SCRATCH = {
 SEMAPHORES = ["ld", "sent", "a1", "a2", "a3", "a4"]
 LIMIT = 256
 PORT = 120
-SPARE = 4
+SPARE = 2
 SPARE_LONE = 10
 ORDER = ((0, 0), (1, 0), (0, 1), (1, 1))
 CACHE = {}
@@ -126,13 +126,22 @@ def make_sends(cores, dead):
                 orphans.append((unit[g, hf], hf, p // 16, g % 2, True))
             if mate[g] is None:
                 orphans.append((unit[g, hf], hf, g // 16, g % 2, False))
+    hub = dict(relay)
+    for g in chips:
+        if mate[g] is not None and len(F[g]) + len(F[mate[g]]) < 4:
+            hub[g // 16, g % 2] = g
+
+    def kind(g, j):
+        if mate[g] is None or j % 4 < 2 or (j % 4 == 3 and j // 4 not in F[g]):
+            return "L"
+        return "E" if j % 4 == 2 else "F"
 
     def layout(g, labels, shed):
         P = len(peers[g])
         m = mate[g]
         hole = {unit[g, 0], unit[g, 1]} | set(F[g].values())
         base = [3 + 1 + (1 if m is None else 0)] * 8
-        typ = ["L" if (m is None or j % 4 < 2) else "E" for j in range(8)]
+        typ = [kind(g, j) for j in range(8)]
         if m is not None:
             hole |= {unit[m, 0], unit[m, 1]} | set(F[m].values())
             for hf in (0, 1):
@@ -142,10 +151,7 @@ def make_sends(cores, dead):
                 if hf in F[m]:
                     base[4 * hf + 1] += UB * (P + 7)
             nat = [1 + P + 4] * 2
-            pin = 5 + ((g // 16, g % 2) in relay)
-            if len(F[g]) + len(F[m]) < 4:
-                for j in (0, 1, 4, 5):
-                    base[j] += UB * SPARE
+            pin = 5 + (hub.get((g // 16, g % 2), g) != g)
         else:
             nat = [P - 1 + 4 + SPARE_LONE] * 2
             pin = 0
@@ -169,6 +175,9 @@ def make_sends(cores, dead):
         return (la, set()), (lm, {hf} if rm else set())
 
     plain = {g: solve(*layout(g, {}, set()), LIMIT) for g in chips}
+    for g in hub.values():
+        if mate[g] is not None:
+            plain[g] = solve(*layout(g, {unit[o, 0]: ("L", None, SPARE * UB) for o in peers[g]}, set()), LIMIT)
     cand = {}
     for i, o in enumerate(orphans):
         for a in chips:
@@ -217,6 +226,12 @@ def make_sends(cores, dead):
 
     jobs = {}
     load = {c: 0 for c in cores}
+    count = {c: 0 for c in cores}
+    hold = {}
+    for g in hub.values():
+        if mate[g] is not None:
+            for o in peers[g]:
+                hold[owner[g, unit[o, 0]]] = hold.get(owner[g, unit[o, 0]], 0) + SPARE * UB
     pout, pin = {}, {}
     chipout = {g: 0 for g in chips}
 
@@ -225,6 +240,7 @@ def make_sends(cores, dead):
         sg, sh = src // 8, src % 8 // 4
         for d in dsts:
             load[src] += n
+            count[src] += 1
             if d // 8 != sg:
                 chipout[sg] += n
                 if d // 8 != mate[sg]:
@@ -278,8 +294,8 @@ def make_sends(cores, dead):
         add(3, owner[m, u], UB * u, UB, [owner[d, u] for d in peers[m]])
     for g in chips:
         m = mate[g]
-        r = relay.get((g // 16, g % 2))
-        for hf in (0, 1):
+        r = hub.get((g // 16, g % 2))
+        for hf in sorted((0, 1), key=lambda hf: -pout.get((g, hf), 0)):
             u = unit[g, hf]
             other = [8 * g + 4 * (1 - hf) + k for k in range(4)]
             if m is None:
@@ -288,7 +304,7 @@ def make_sends(cores, dead):
                     add(3, c, UB * u, UB, [d])
                 continue
             en = 8 * g + 4 * hf + 2
-            add(2, en, UB * u, UB, [8 * m + 4 * hf] + other + ([owner[r, u]] if r is not None else []))
+            add(2, en, UB * u, UB, [8 * m + 4 * hf] + other + ([owner[r, u]] if r not in (None, g) else []))
             for d in peers[g]:
                 if d == r:
                     continue
@@ -297,10 +313,11 @@ def make_sends(cores, dead):
                 elif load[en] + UB <= LIMIT:
                     c = en
                 else:
-                    c = min((8 * g + 4 * hf + k for k in (0, 1, 3)), key=lambda k: load[k])
-                add(2 if c % 4 > 1 else 3, c, UB * u, UB, [owner[d, u]])
+                    c = min((k for k in (en - 2, en - 1, en + 1) if load[k] + hold.get(k, 0) + UB <= LIMIT),
+                            key=lambda k: (count[k], load[k]))
+                add(3 if kind(g, c % 8) == "L" else 2, c, UB * u, UB, [owner[d, u]])
     for h, q in sorted({(g // 16, g % 2) for g in chips}):
-        r = min((g for g in chips if (g // 16, g % 2) == (h, q)), key=lambda g: chipout[g])
+        r = hub.get((h, q), min((g for g in chips if (g // 16, g % 2) == (h, q)), key=lambda g: chipout[g]))
         while True:
             o = max(peers[r], key=lambda d: chipout[d])
             if chipout[o] - UB < chipout[r] + UB:
@@ -308,16 +325,18 @@ def make_sends(cores, dead):
             opts = []
             for (hop, src, b0, n), dsts in jobs.items():
                 k = owner.get((r, b0 // UB))
-                if hop == 2 and src // 8 == o and n == UB and k in dsts and (mate[r] is None or k % 4 < 2):
+                if src // 8 == o and n == UB and hop < 4 and k is not None and kind(r, k % 8) == "L" and any(
+                        k in jobs.get((2, 8 * o + j, b0, n), ()) for j in range(8)):
                     rest = [d for d in dsts if d // 8 in peers[o] and d // 8 != r
                             and pin[d // 8, k % 8 // 4] + UB <= PORT]
                     if rest and load[k] + UB <= LIMIT and pout[r, k % 8 // 4] + UB <= PORT:
-                        opts.append(((3, k, b0, n) not in jobs, -load[src], load[k], src, b0, rest[-1], k))
+                        opts.append(((3, k, b0, n) not in jobs, -load[src], load[k], hop, src, b0, rest[-1], k))
             if not opts:
                 break
-            src, b0, d, k = min(opts)[3:]
-            jobs[2, src, b0, UB].remove(d)
+            hop, src, b0, d, k = min(opts)[3:]
+            jobs[hop, src, b0, UB].remove(d)
             load[src] -= UB
+            count[src] -= 1
             chipout[o] -= UB
             pout[o, src % 8 // 4] -= UB
             pin[d // 8, src % 8 // 4] -= UB

import concourse.bass as bass

BLK = 16
NRANK = 248
UB = 4
SCRATCH = {
    "G": ("sbuf", [128, NRANK * BLK], "float32"),
}
SEMAPHORES = ["ld", "sent", "a1", "a2", "a3", "a4"]
LIMIT = 256
PORT = 120
SPARE = 2
SPARE_LONE = 10
ORDER = ((0, 0), (1, 0), (0, 1), (1, 1))
CACHE = {}


def solve(segs, labels, base, typ, nat, pin, limit):
    fwd = 7 * UB
    haslab = [any(u in labels for u in s) for s in segs]
    total = sum(len(s) for s in segs)

    def fits(j, us, load):
        for u in us:
            if u in labels:
                t, hf, extra = labels[u]
                if typ[j] != t or (hf is not None and j // 4 != hf):
                    return None
                load += extra
        load += fwd * len(us)
        return load if load <= limit else None

    def search(twos, helpers):
        load = list(base)
        for hf in (0, 1):
            load[4 * hf + 2] += UB * (pin if helpers else nat[hf])
        runs = {}
        failed = set()

        def rec(si, off, last, used, pend, two, left):
            if si == len(segs):
                if used != 255 or pend is not None:
                    return False
                return not helpers or all(
                    sum((limit - load[j]) // UB for j in range(4 * hf, 4 * hf + 4)) >= nat[hf] - pin for hf in (0, 1))
            seg = segs[si]
            if off == len(seg):
                return rec(si + 1, 0, -1, used, pend, two, left)
            key = (si, off, last, used, pend, two)
            if helpers:
                key += (sum(load[:4]),)
            if key in failed:
                return False
            room = len(seg) - off
            free = [j for j in range(8) if not used >> j & 1]
            slack = sum((limit - load[j]) // fwd for j in free) + (pend[1] if pend else 0) - left
            if slack >= 0:
                if pend and pend[1] <= room:
                    j, w = pend
                    old = load[j]
                    new = fits(j, seg[off:off + w], old)
                    if new is not None:
                        load[j] = new
                        runs[j].append((seg[off], w))
                        if rec(si, off + w, last, used, None, two, left - w):
                            return True
                        runs[j].pop()
                        load[j] = old
                for j in free:
                    if not haslab[si] and j < last:
                        continue
                    old = load[j]
                    cap = (limit - old) // fwd
                    for w in range(min(cap, room), max(0, cap - slack - 1), -1):
                        new = fits(j, seg[off:off + w], old)
                        if new is None:
                            continue
                        load[j] = new
                        runs[j] = [(seg[off], w)]
                        if rec(si, off + w, j, used | 1 << j, pend, two, left - w):
                            return True
                    if two < twos and pend is None:
                        for w in range(min(cap // 2, room), 1, -1):
                            if 2 * w < cap - slack:
                                break
                            new = fits(j, seg[off:off + w], old)
                            if new is None or new + fwd * w > limit:
                                continue
                            load[j] = new
                            runs[j] = [(seg[off], w)]
                            if rec(si, off + w, j, used | 1 << j, (j, w), two + 1, left - w):
                                return True
                    load[j] = old
                    runs.pop(j, None)
            failed.add(key)
            return False

        return runs if rec(0, 0, -1, 0, None, 0, total) else None

    for n, cost in enumerate(ORDER):
        if pin == 0 and cost[1] == 0:
            continue
        runs = search(cost[0], cost[1] == 1)
        if runs is not None:
            return n, runs
    return None, None


def make_sends(cores, dead):
    rank = {c: i for i, c in enumerate(cores)}
    chips = sorted({c // 8 for c in cores})
    nunit = len(cores) // UB
    unit = {(g, hf): rank[8 * g + 4 * hf] // UB for g in chips for hf in (0, 1)}
    mate = {g: (g ^ 1 if g ^ 1 in chips else None) for g in chips}
    peers = {g: [d for d in chips if d != g and d // 16 == g // 16 and d % 2 == g % 2] for g in chips}
    lone = [g for g in chips if mate[g] is None]
    relay = {(g // 16, g % 2): g for g in lone}
    F = {g: {} for g in chips}
    orphans = []
    for g in chips:
        p = g ^ 16
        for hf in (0, 1):
            if p in chips and mate[p] is not None:
                F[p][hf] = unit[g, hf]
            else:
                orphans.append((unit[g, hf], hf, p // 16, g % 2, True))
            if mate[g] is None:
                orphans.append((unit[g, hf], hf, g // 16, g % 2, False))
    hub = dict(relay)
    for g in chips:
        if mate[g] is not None and len(F[g]) + len(F[mate[g]]) < 4:
            hub[g // 16, g % 2] = g

    def kind(g, j):
        if mate[g] is None or j % 4 < 2 or (j % 4 == 3 and j // 4 not in F[g]):
            return "L"
        return "E" if j % 4 == 2 else "F"

    def layout(g, labels, shed):
        P = len(peers[g])
        m = mate[g]
        hole = {unit[g, 0], unit[g, 1]} | set(F[g].values())
        base = [3 + 1 + (1 if m is None else 0)] * 8
        typ = [kind(g, j) for j in range(8)]
        if m is not None:
            hole |= {unit[m, 0], unit[m, 1]} | set(F[m].values())
            for hf in (0, 1):
                if hf in F[g]:
                    base[4 * hf + 3] += UB * (1 + (1 if hf in shed else P) + 7)
                base[4 * hf] += UB * (P + 7)
                if hf in F[m]:
                    base[4 * hf + 1] += UB * (P + 7)
            nat = [1 + P + 4] * 2
            pin = 5 + (hub.get((g // 16, g % 2), g) != g)
        else:
            nat = [P - 1 + 4 + SPARE_LONE] * 2
            pin = 0
        segs = []
        for u in range(nunit):
            if u in hole:
                continue
            if segs and segs[-1][-1] == u - 1:
                segs[-1].append(u)
            else:
                segs.append([u])
        return segs, labels, base, typ, nat, pin

    def adoption(a, orphan):
        u, hf, h, q, foreign = orphan
        m = mate[a]
        ra, rm = (h, q) in relay, (h, 1 - q) in relay
        ea = UB * ((1 + (1 if ra else len(peers[a]))) if foreign else 1)
        la = {u: ("E", hf if ra and foreign else None, ea)}
        lm = {u: ("L", hf if rm else None, UB * len(peers[m]))}
        return (la, set()), (lm, {hf} if rm else set())

    plain = {g: solve(*layout(g, {}, set()), LIMIT) for g in chips}
    for g in hub.values():
        if mate[g] is not None:
            plain[g] = solve(*layout(g, {unit[o, 0]: ("L", None, SPARE * UB) for o in peers[g]}, set()), LIMIT)
    cand = {}
    for i, o in enumerate(orphans):
        for a in chips:
            if a // 16 == o[2] and a % 2 == o[3] and mate[a] is not None:
                (la, sa), (lm, sm) = adoption(a, o)
                ca = solve(*layout(a, la, sa), LIMIT)
                cm = solve(*layout(mate[a], lm, sm), LIMIT)
                if ca[0] is not None and cm[0] is not None:
                    cand[i, a] = (ca, cm, ca[0] + cm[0] - plain[a][0] - plain[mate[a]][0])
    pick = {"cost": None, "sel": None}

    def match(i, sel, cost):
        if pick["cost"] is not None and cost >= pick["cost"]:
            return
        if i == len(orphans):
            pick["cost"], pick["sel"] = cost, dict(sel)
            return
        for a in chips:
            if (i, a) in cand and a not in sel.values() and mate[a] not in sel.values():
                sel[i] = a
                match(i + 1, sel, cost + cand[i, a][2])
                del sel[i]

    match(0, {}, 0)
    adopt = pick["sel"]
    runs = {g: plain[g][1] for g in chips}
    shed = {g: set() for g in chips}
    for i, a in adopt.items():
        runs[a], runs[mate[a]] = cand[i, a][0][1], cand[i, a][1][1]
        shed[mate[a]] = adoption(a, orphans[i])[1][1]
    for r in lone:
        lab = {}
        for i, a in adopt.items():
            u, hf, h, q, foreign = orphans[i]
            if foreign and relay.get((h, q)) == r:
                lab[u] = ("L", hf, UB * (len(peers[r]) - 1))
            if relay.get((h, 1 - q)) == r:
                lab[F[mate[a]][hf]] = ("L", hf, UB * (len(peers[r]) - 1))
        runs[r] = solve(*layout(r, lab, set()), LIMIT)[1]
    owner = {}
    for g in chips:
        for j, rs in runs[g].items():
            for u0, w in rs:
                for u in range(u0, u0 + w):
                    owner[g, u] = 8 * g + j

    jobs = {}
    load = {c: 0 for c in cores}
    count = {c: 0 for c in cores}
    hold = {}
    for g in hub.values():
        if mate[g] is not None:
            for o in peers[g]:
                hold[owner[g, unit[o, 0]]] = hold.get(owner[g, unit[o, 0]], 0) + SPARE * UB
    pout, pin = {}, {}
    chipout = {g: 0 for g in chips}

    def add(hop, src, b0, n, dsts):
        jobs.setdefault((hop, src, b0, n), []).extend(dsts)
        sg, sh = src // 8, src % 8 // 4
        for d in dsts:
            load[src] += n
            count[src] += 1
            if d // 8 != sg:
                chipout[sg] += n
                if d // 8 != mate[sg]:
                    pout[sg, sh] = pout.get((sg, sh), 0) + n
                    pin[d // 8, sh] = pin.get((d // 8, sh), 0) + n

    def sibs(c, half=None):
        return [8 * (c // 8) + k for k in range(8) if 8 * (c // 8) + k != c and (half is None or k // 4 == half)]

    land = {}
    for g in chips:
        for hf, u in F[g].items():
            land.setdefault(u, []).append(8 * g + 4 * hf + 3)
    for i, a in adopt.items():
        land.setdefault(orphans[i][0], []).append(owner[a, orphans[i][0]])
    for g in chips:
        m = mate[g]
        for j in range(8):
            c = 8 * g + j
            add(1, c, rank[c], 1, sibs(c, j // 4) + land[unit[g, j // 4]])
            for u0, w in runs[g][j]:
                add(4, c, UB * u0, UB * w, sibs(c))
        if m is None:
            continue
        r = relay.get((g // 16, g % 2))
        for hf in (0, 1):
            if hf in F[g]:
                u, c = F[g][hf], 8 * g + 4 * hf + 3
                if hf in shed[g]:
                    add(2, c, UB * u, UB, [8 * m + 4 * hf + 1, owner[r, u]] + sibs(c))
                    add(3, owner[r, u], UB * u, UB, [owner[d, u] for d in peers[g] if d != r])
                else:
                    add(2, c, UB * u, UB, [8 * m + 4 * hf + 1] + [owner[d, u] for d in peers[g]] + sibs(c))
            for u, c in ((unit[m, hf], 8 * g + 4 * hf), (F[m].get(hf), 8 * g + 4 * hf + 1)):
                if u is not None:
                    add(3, c, UB * u, UB, [owner[d, u] for d in peers[g]] + sibs(c))
    skip = {}
    for i, a in adopt.items():
        u, hf, h, q, foreign = orphans[i]
        m = mate[a]
        r = relay.get((h, q))
        dsts = [owner[m, u]]
        if foreign and r is not None:
            dsts.append(owner[r, u])
            add(3, owner[r, u], UB * u, UB, [owner[d, u] for d in peers[a] if d != r])
        elif foreign:
            dsts += [owner[d, u] for d in peers[a]]
        else:
            skip[u] = a
        add(2, owner[a, u], UB * u, UB, dsts)
        add(3, owner[m, u], UB * u, UB, [owner[d, u] for d in peers[m]])
    for g in chips:
        m = mate[g]
        r = hub.get((g // 16, g % 2))
        for hf in sorted((0, 1), key=lambda hf: -pout.get((g, hf), 0)):
            u = unit[g, hf]
            other = [8 * g + 4 * (1 - hf) + k for k in range(4)]
            if m is None:
                for d in other + [owner[d, u] for d in peers[g] if d != skip.get(u)]:
                    c = min((8 * g + 4 * hf + k for k in range(4)), key=lambda k: load[k])
                    add(3, c, UB * u, UB, [d])
                continue
            en = 8 * g + 4 * hf + 2
            add(2, en, UB * u, UB, [8 * m + 4 * hf] + other + ([owner[r, u]] if r not in (None, g) else []))
            for d in peers[g]:
                if d == r:
                    continue
                if pout.get((g, hf), 0) + UB > PORT:
                    c = min((8 * g + 4 * (1 - hf) + k for k in (0, 1)), key=lambda k: load[k])
                elif load[en] + UB <= LIMIT:
                    c = en
                else:
                    c = min((k for k in (en - 2, en - 1, en + 1) if load[k] + hold.get(k, 0) + UB <= LIMIT),
                            key=lambda k: (count[k], load[k]))
                add(3 if kind(g, c % 8) == "L" else 2, c, UB * u, UB, [owner[d, u]])
    for h, q in sorted({(g // 16, g % 2) for g in chips}):
        r = hub.get((h, q), min((g for g in chips if (g // 16, g % 2) == (h, q)), key=lambda g: chipout[g]))
        while True:
            o = max(peers[r], key=lambda d: chipout[d])
            if chipout[o] - UB < chipout[r] + UB:
                break
            opts = []
            for (hop, src, b0, n), dsts in jobs.items():
                k = owner.get((r, b0 // UB))
                if src // 8 == o and n == UB and hop < 4 and k is not None and kind(r, k % 8) == "L" and any(
                        k in jobs.get((2, 8 * o + j, b0, n), ()) for j in range(8)):
                    rest = [d for d in dsts if d // 8 in peers[o] and d // 8 != r
                            and pin[d // 8, k % 8 // 4] + UB <= PORT]
                    if rest and load[k] + UB <= LIMIT and pout[r, k % 8 // 4] + UB <= PORT:
                        opts.append(((3, k, b0, n) not in jobs, -load[src], load[k], hop, src, b0, rest[-1], k))
            if not opts:
                break
            hop, src, b0, d, k = min(opts)[3:]
            jobs[hop, src, b0, UB].remove(d)
            load[src] -= UB
            count[src] -= 1
            chipout[o] -= UB
            pout[o, src % 8 // 4] -= UB
            pin[d // 8, src % 8 // 4] -= UB
            add(3, k, b0, UB, [d])
    return [(hop, src, b0, n, dsts) for (hop, src, b0, n), dsts in sorted(jobs.items()) if dsts]


def compile_sends(sends):
    calls = {}
    for hop, src, b0, n, dsts in sends:
        for k in range(0, len(dsts), 16):
            calls.setdefault((src, hop, n), []).append((b0, list(dsts[k:k + 16])))
    prog = {}
    arrive = {}
    sent = {}
    for (src, hop, n), trs in sorted(calls.items()):
        off = [tr for tr in trs if any(d // 8 != src // 8 for d in tr[1])]
        on = [tr for tr in trs if tr not in off]
        out = []
        for group, base in ((off, 0), (on, 8)):
            if not group:
                continue
            assert len(group) <= 8
            e = 8
            while e * len(group) > 8:
                e //= 2
            for i, (b0, dsts) in enumerate(group):
                mask = ((1 << e) - 1) << (base + i * e)
                out.append((b0, dsts, mask, e))
                sent[src] = sent.get(src, 0) + e
                for d in dsts:
                    arrive[d, hop] = arrive.get((d, hop), 0) + e
        prog.setdefault(src, {}).setdefault(hop, []).append((n, out))
    return prog, arrive, sent


def rank_program(g, core, T, topo):
    rank = T.rank_of(core)
    if rank is None:
        return
    if "plan" not in CACHE:
        CACHE["plan"] = compile_sends(make_sends(list(T.cores), T.tables["DEAD"]))
    prog, arrive, sent = CACHE["plan"]
    G = T.G
    sems = {1: T.sem.a1, 2: T.sem.a2, 3: T.sem.a3, 4: T.sem.a4}
    g.dma_start(G[:, rank * BLK:(rank + 1) * BLK], T.x[:, :]).then_inc(T.sem.ld, 16)
    g.wait_ge(T.sem.ld, 16)
    for hop in (1, 2, 3, 4):
        if hop > 1 and arrive.get((core, hop - 1), 0):
            g.wait_ge(sems[hop - 1], arrive[core, hop - 1])
        for n, trs in prog.get(core, {}).get(hop, []):
            lst = []
            for b0, dsts, mask, e in trs:
                ap = G[:, b0 * BLK:(b0 + n) * BLK]
                ids = []
                for d in dsts:
                    rid, pid = topo.addr(d, core)
                    ids.append(bass.DstId(rid=rid, pnc=pid))
                lst.append(bass.RemoteDMATransfer(dst_ids=ids, dma_engine_mask=mask, remote_sem=sems[hop],
                                                  srcs=[ap], dsts=[ap for d in dsts]))
            g.remote_dma_fused(lst, local_sem=T.sem.sent)
    if arrive.get((core, 4), 0):
        g.wait_ge(sems[4], arrive[core, 4])
    if sent.get(core, 0):
        g.wait_ge(T.sem.sent, sent[core])
    g.dma_start(T.y[:, :], G[:, :]).then_inc(T.sem.ld, 16)
    g.wait_ge(T.sem.ld, 32)
